import numpy as np
import ml_dtypes


def mxq(x, axis, fmt="e4m3"):
    dtype, down = {"e4m3": (ml_dtypes.float8_e4m3fn, 7), "e5m2": (ml_dtypes.float8_e5m2, 14)}[fmt]
    v = np.moveaxis(np.asarray(x, np.float32).astype(ml_dtypes.bfloat16).astype(np.float64), axis, -1)
    blocks = v.reshape(v.shape[:-1] + (-1, 32))
    amax = np.abs(blocks).max(-1, keepdims=True)
    byte = np.maximum(np.where(amax > 0, np.frexp(amax)[1] - 1 + 127, 0) - down, 1)
    scale = np.exp2(byte - 127.0)
    codes = (blocks / scale).astype(np.float32).astype(dtype).astype(np.float64)
    return np.moveaxis((codes * scale).reshape(v.shape), -1, axis)


WIDE = False


def mx_kscale(k):
    if not WIDE:
        return np.ones(k)
    levels = np.array([10, -10, 5, -5, 0])
    if k % 512:
        return np.exp2(np.random.permutation(np.resize(levels, k // 32))).repeat(32)
    a = np.empty((k // 512, 16))
    for p in range(k // 512):
        a[p, :8] = np.random.permutation(np.resize(levels, 8))
        for g in range(8):
            far = levels[np.abs(levels - a[p, g]) >= 10]
            a[p, g + 8] = far[np.random.randint(len(far))]
    return np.exp2(a.ravel()).repeat(32)


BF16 = ml_dtypes.bfloat16


def bf(x):
    return np.asarray(x, np.float32).astype(BF16)


def f64(x):
    return np.asarray(x).astype(np.float64)

def planes(Y):
    n, m = Y.shape
    b = f64(bf(Y)).reshape(n // 32, 32, m)
    amax = np.abs(b).max(1)
    byte = np.clip(np.where(amax > 0, np.frexp(amax)[1] - 1 + 127 - 7, 1), 1, 254)
    codes = (b * np.exp2(127.0 - byte)[:, None, :]).reshape(n, m).astype(np.float32).astype(ml_dtypes.float8_e4m3fn).view(np.uint8)
    words = codes.reshape(n // 512, 128, 4, m).transpose(0, 1, 3, 2)
    return np.ascontiguousarray(words), np.ascontiguousarray(byte.astype(np.uint8).reshape(n // 512, 16, m))


N, DS, DT, V = 512, 1024, 1024, 2048


def head_probs(logits):
    p = np.exp(logits - logits.max(axis=-1, keepdims=True))
    return p / p.sum(axis=-1, keepdims=True)


def setup_inputs():
    a, b, u = mx_kscale(DS), mx_kscale(DT), mx_kscale(V)
    return {
        "hs": bf(np.random.standard_normal((N, DS)) * 1.3 * a),
        "ht": bf(np.random.standard_normal((N, DT)) * 1.3 * b),
        "ws": bf(np.random.standard_normal((DS, V)) / np.sqrt(DS) / a[:, None]),
        "wt": bf(np.random.standard_normal((DT, V)) / np.sqrt(DT) / b[:, None]),
        "c": bf((1.0 + 0.1 * np.random.standard_normal(V)) * u),
        "wb": bf(np.random.standard_normal((V, DS)) / np.sqrt(V) / u[:, None]),
    }


def core(hs, ht, ws, wt, c, wb):
    vocab = ws.shape[1]
    s = head_probs(mxq(f64(hs), 1, "e4m3") @ mxq(f64(ws), 0, "e4m3"))
    t = head_probs(mxq(f64(ht), 1, "e4m3") @ mxq(f64(wt), 0, "e4m3"))
    r = -np.log(0.6 + 0.4 * t / s)
    m = np.sum(s * r, axis=-1, keepdims=True)
    e = (0.6 * vocab) * s * (r - m)
    ec = e * f64(c)[None, :]
    return mxq(ec, 1, "e4m3") @ mxq(f64(wb), 0, "e4m3")


def reference(hs, ht, ws, wt, c, wb):
    R_out = core(hs, ht, ws, wt, c, wb)
    words, scales = planes(R_out)
    return R_out, words, scales

@@ -1,0 +1,516 @@
+from contextlib import ExitStack
+
+import concourse.mybir as mybir
+from concourse.masks import make_identity
+
+F32 = mybir.dt.float32
+BF16 = mybir.dt.bfloat16
+U32 = mybir.dt.uint32
+I32 = mybir.dt.int32
+U8 = mybir.dt.uint8
+FP8X4 = mybir.dt.float8_e4m3fn_x4
+ACT = mybir.ActivationFunctionType
+ALU = mybir.AluOpType
+AX = mybir.AxisListType
+
+P = 128
+PACK = 4
+KP = 512
+N, D, V, O = 512, 1024, 2048, 1024
+TILES = N // P
+CH = 512
+CHUNKS = V // CH
+DG = D // KP
+VG = V // KP
+HALVES = O // CH
+FLOPS = 2 * N * V * (D + D) + 2 * N * V * O
+
+
+def tile_jsdlogitgradgainprojection_kernel(tc, hs, ht, ws, wt, c, wb, out_0, out_1, out_2):
+    nc = tc.nc
+    with ExitStack() as ctx:
+        keep = ctx.enter_context(tc.tile_pool(name="keep", bufs=1))
+        pool = ctx.enter_context(tc.tile_pool(name="work", bufs=2))
+        psum = ctx.enter_context(tc.psum_pool(name="psum", bufs=8))
+
+        ident = keep.tile([P, P], F32, name="ident")
+        make_identity(nc, ident[:])
+
+        ctx.enter_context(tc.manual_schedule())
+
+        def bank():
+            b = psum.tile([P, KP], F32, name="bank", tag="bank")
+            return b
+
+        nmx = keep.tile([P, 32], F32, name="nmx")
+        zacc = keep.tile([P, 32], F32, name="zacc")
+        ebias = keep.tile([P, 16], F32, name="ebias")
+
+        es = [keep.tile([P, V], F32, name="es%d" % t) for t in range(TILES)]
+        ee = [keep.tile([P, V], F32, name="ee%d" % t) for t in range(TILES)]
+
+        raws = {}
+
+        def load_w(x, c_, g):
+            src = ws if x == 0 else wt
+            r = pool.tile([P, PACK, CH], BF16, name="raw", tag="raw", bufs=8, align_bytes=64)
+            nc.sync.dma_start(
+                out=r[:],
+                in_=src[KP * g : KP * (g + 1), CH * c_ : CH * (c_ + 1)].rearrange("(p j) w -> p j w", j=PACK),
+            )
+            raws[x, c_, g] = r
+
+        hraw = [pool.tile([P, TILES, D], BF16, name="hraw%d" % x, tag="big", bufs=2, align_bytes=64) for x in (0, 1)]
+
+        def load_h(x, half):
+            src = (hs if x == 0 else ht).rearrange("(p t) k -> p t k", t=TILES)
+            nc.sync.dma_start(
+                out=hraw[x][:, 2 * half : 2 * half + 2, :], in_=src[:, 2 * half : 2 * half + 2, :]
+            )
+
+        wbraw = {}
+
+        def load_wb(g):
+            r = pool.tile([P, PACK, O], BF16, name="wbraw", tag="wbraw", bufs=2, align_bytes=64)
+            nc.sync.dma_start(out=r[:], in_=wb[KP * g : KP * (g + 1), :].rearrange("(p j) w -> p j w", j=PACK))
+            wbraw[g] = r
+
+        cb = keep.tile([P, V], BF16, name="cb")
+
+        grps = {}
+
+        def new_grp(key):
+            q = pool.tile([P, CH * PACK], BF16, name="grp", tag="grp", bufs=6, align_bytes=64)
+            grps[key] = q
+
+        def views(dst, src, lo, hi):
+            d = dst[:, PACK * lo : PACK * hi].rearrange("p (c i t) -> p c t i", i=4, t=PACK)
+            s = src[:, :, lo:hi].rearrange("p t (c i) -> p c t i", i=4)
+            return d, s
+
+        def il_w(x, c_, g, eng, lo=0, hi=CH):
+            if (x, c_, g) not in grps:
+                new_grp((x, c_, g))
+            d, s = views(grps[x, c_, g], raws[x, c_, g], lo, hi)
+            if x == 0:
+                nc.vector.tensor_scalar(out=d, in0=s, scalar1=-1.0, scalar2=None, op0=ALU.mult)
+            elif eng == "v":
+                nc.vector.tensor_copy(out=d, in_=s)
+            else:
+                nc.scalar.copy(out=d, in_=s)
+
+        wcode, wscale = {}, {}
+
+        def q_w(x, c_, g):
+            if (x, c_) not in wcode:
+                a = pool.tile([P, DG * CH], U32, name="wcode%d" % x, tag="wcode%d" % x, bufs=2, align_bytes=64)
+                b = pool.tile([P, DG * CH], U8, name="wscale%d" % x, tag="wscale%d" % x, bufs=2, align_bytes=64)
+                wcode[x, c_], wscale[x, c_] = a, b
+            cols = slice(CH * g, CH * (g + 1))
+            nc.vector.quantize_mx(
+                out=wcode[x, c_][:, cols].bitcast(FP8X4), scales=wscale[x, c_][:, cols], in_=grps[x, c_, g][:]
+            )
+
+        bcode = [keep.tile([P, O], U32, name="bcode%d" % g, align_bytes=64) for g in range(VG)]
+        bscale = [keep.tile([P, O], U8, name="bscale%d" % g, align_bytes=64) for g in range(VG)]
+
+        def il_b(i, eng):
+            g, h = i // 2, i % 2
+            new_grp(("b", i))
+            d = grps["b", i][:].rearrange("p (c i t) -> p c t i", i=4, t=PACK)
+            s = wbraw[g][:, :, CH * h : CH * (h + 1)].rearrange("p t (c i) -> p c t i", i=4)
+            if eng == "v":
+                nc.vector.tensor_copy(out=d, in_=s)
+            else:
+                nc.scalar.copy(out=d, in_=s)
+
+        def q_b(i):
+            g, h = i // 2, i % 2
+            cols = slice(CH * h, CH * (h + 1))
+            nc.vector.quantize_mx(out=bcode[g][:, cols].bitcast(FP8X4), scales=bscale[g][:, cols], in_=grps["b", i][:])
+
+        hcode, hscale, hgrp = {}, {}, {}
+
+        def tr_h(x, t):
+            words = hraw[x][:].bitcast(F32)
+            b = bank()
+            v = b[:].rearrange("p (g u r) -> p g u r", g=DG, u=2)
+            for g in range(DG):
+                for u in range(2):
+                    nc.tensor.transpose(v[:, g, u, :], words[:, t, 256 * g + u : 256 * (g + 1) : 2], ident[:])
+            q = pool.tile([P, DG * P * PACK], BF16, name="hgrp", tag="hgrp", bufs=3, align_bytes=64)
+            nc.scalar.copy(
+                out=q[:].bitcast(F32).rearrange("p (g r u) -> p g r u", g=DG, u=2),
+                in_=b[:].rearrange("p (g u r) -> p g r u", g=DG, u=2),
+            )
+            hgrp[x, t] = q
+
+        def q_h(x, t):
+            a = keep.tile([P, DG * P], U32, name="hcode%d%d" % (x, t), align_bytes=64)
+            b = keep.tile([P, DG * P], U8, name="hscale%d%d" % (x, t), align_bytes=64)
+            hcode[x, t], hscale[x, t] = a, b
+            nc.vector.quantize_mx(out=a[:].bitcast(FP8X4), scales=b[:], in_=hgrp[x, t][:])
+
+        def mm_h(b, x, t, c_, g, start, stop):
+            rows = slice(P * g, P * (g + 1))
+            cols = slice(CH * g, CH * (g + 1))
+            nc.tensor.matmul_mx(
+                out=b[:],
+                lhsT=hcode[x, t][:, rows].bitcast(FP8X4),
+                lhsT_scale=hscale[x, t][:, rows],
+                rhs=wcode[x, c_][:, cols].bitcast(FP8X4),
+                rhs_scale=wscale[x, c_][:, cols],
+                start=start,
+                stop=stop,
+            )
+
+        units = {}
+
+        def unit_pe(t, j):
+            bn, bt, bd = bank(), bank(), bank()
+            for b, x in ((bn, 0), (bt, 1)):
+                for g in range(DG):
+                    mm_h(b, x, t, j, g, g == 0, g == DG - 1)
+            order = [(0, 0), (0, 1), (1, 0), (1, 1)]
+            for i, (x, g) in enumerate(order):
+                mm_h(bd, x, t, j, g, i == 0, i == 3)
+            units[t, j] = (bn, bt, bd)
+
+        def unit_max(t, j):
+            bn, bt, bd = units[t, j]
+            k = CHUNKS * t + j
+            nc.vector.tensor_reduce(out=nmx[:, k : k + 1], in_=bn[:], axis=AX.X, op=ALU.min)
+            nc.vector.tensor_reduce(out=nmx[:, 16 + k : 17 + k], in_=bt[:], axis=AX.X, op=ALU.max, negate=True)
+            nc.gpsimd.tensor_tensor(
+                out=ebias[:, k : k + 1], in0=nmx[:, 16 + k : 17 + k], in1=nmx[:, k : k + 1], op=ALU.subtract
+            )
+
+        def unit_exp(t, j):
+            bn, bt, bd = units[t, j]
+            k = CHUNKS * t + j
+            cols = slice(CH * j, CH * (j + 1))
+            nc.scalar.activation(
+                out=es[t][:, cols], in_=bn[:], func=ACT.Exp, bias=nmx[:, k : k + 1], scale=-1.0,
+                accum_out=zacc[:, k : k + 1],
+            )
+            junk = pool.tile([P, CH], F32, name="junk", tag="junk", bufs=2)
+            nc.scalar.activation(
+                out=junk[:], in_=bt[:], func=ACT.Exp, bias=nmx[:, 16 + k : 17 + k], scale=1.0,
+                accum_out=zacc[:, 16 + k : 17 + k],
+            )
+
+        def unit_ratio(t, j):
+            bn, bt, bd = units[t, j]
+            k = CHUNKS * t + j
+            cols = slice(CH * j, CH * (j + 1))
+            nc.scalar.activation(out=ee[t][:, cols], in_=bd[:], func=ACT.Exp, bias=ebias[:, k : k + 1], scale=1.0)
+
+        load_w(0, 0, 0)
+        load_w(0, 0, 1)
+        load_h(0, 0)
+        load_w(1, 0, 0)
+        load_w(1, 0, 1)
+        load_h(1, 0)
+        load_h(0, 1)
+        load_h(1, 1)
+        for x in (0, 1):
+            for g in (0, 1):
+                load_w(x, 1, g)
+        load_wb(0)
+
+        il_w(0, 0, 0, "v")
+        il_w(0, 0, 1, "v")
+        q_w(0, 0, 0)
+        q_w(0, 0, 1)
+        tr_h(0, 0)
+        il_w(1, 0, 0, "s")
+        il_w(1, 0, 1, "v")
+        tr_h(1, 0)
+        q_h(0, 0)
+        q_h(1, 0)
+        q_w(1, 0, 1)
+        q_w(1, 0, 0)
+        tr_h(0, 1)
+        tr_h(1, 1)
+        il_w(0, 1, 0, "v")
+        q_h(0, 1)
+        q_h(1, 1)
+
+        vfill = {}
+        sfill = {}
+        for j in range(CHUNKS):
+            for t in range(TILES):
+                vfill[j, t] = []
+                sfill[j, t] = []
+        vfill[0, 0] += [lambda: q_h(0, 2), lambda: q_h(1, 2)]
+        vfill[0, 1] += [lambda: q_h(0, 3), lambda: q_h(1, 3)]
+        sfill[0, 0] += [lambda: tr_h(0, 2), lambda: tr_h(1, 2), lambda: tr_h(0, 3), lambda: tr_h(1, 3),
+                        lambda: il_w(1, 1, 0, "s")]
+        for j in range(CHUNKS - 1):
+            n = j + 1
+            vfill[j, 0].append(lambda n=n: il_w(0, n, 1, "v"))
+            vfill[j, 1] += [lambda n=n: q_w(0, n, 0), lambda n=n: q_w(1, n, 0)]
+            vfill[j, 2] += [lambda n=n: q_w(0, n, 1), lambda n=n: q_w(1, n, 1)]
+            sfill[j, 0].append(lambda n=n: il_w(1, n, 1, "s", 0, 256))
+            vfill[j, 1].append(lambda n=n: il_w(1, n, 1, "v", 256, 512))
+            if n + 1 < CHUNKS:
+                vfill[j, 3].append(lambda n=n: il_w(0, n + 1, 0, "v"))
+                sfill[j, 3].append(lambda n=n: il_w(1, n + 1, 0, "s"))
+        vfill[2, 2].append(lambda: il_b(0, "v"))
+        vfill[2, 3] += [lambda: q_b(0), lambda: il_b(1, "v")]
+        vfill[3, 0] += [lambda: q_b(1), lambda: il_b(2, "v")]
+        vfill[3, 1] += [lambda: q_b(2), lambda: il_b(3, "v")]
+        sfill[3, 1].append(lambda: il_b(4, "s"))
+        vfill[3, 2] += [lambda: q_b(3)]
+
+        for j in range(CHUNKS):
+            for t in range(TILES):
+                unit_pe(t, j)
+                unit_max(t, j)
+                unit_exp(t, j)
+                for f in sfill[j, t]:
+                    f()
+                unit_ratio(t, j)
+                for f in vfill[j, t]:
+                    f()
+                if t == 1 and j < 2:
+                    for g in (0, 1):
+                        for x in (0, 1):
+                            load_w(x, j + 2, g)
+                    load_wb(j + 1)
+                    if j == 0:
+                        nc.sync.dma_start(out=cb[:], in_=c.partition_broadcast(P))
+                if t == 3 and j == 2:
+                    load_wb(3)
+
+        stat = keep.tile([P, 8, 4], F32, name="stat")
+        nm = keep.tile([P, 8], F32, name="nm")
+        wgt = keep.tile([P, 32], F32, name="wgt")
+        zz = keep.tile([P, 32], F32, name="zz")
+        zr = keep.tile([P, 8], F32, name="zr")
+        rr = keep.tile([P, 8], F32, name="rr")
+        gg = keep.tile([P, 32], F32, name="gg")
+        gs = keep.tile([P, 32], F32, name="gs")
+        rec = keep.tile([P, 16], F32, name="rec")
+        kap = keep.tile([P, 16], F32, name="kap")
+        ff = keep.tile([P, 16], F32, name="ff")
+        nmx3 = nmx[:].rearrange("p (a j) -> p a j", j=4)
+        nc.vector.tensor_reduce(out=nm[:], in_=nmx3, axis=AX.X, op=ALU.min)
+        q_b(4)
+        nc.vector.tensor_tensor(out=stat[:], in0=nm[:].unsqueeze(2).to_broadcast([P, 8, 4]), in1=nmx3, op=ALU.subtract)
+        nc.scalar.activation(out=wgt[:], in_=stat[:].rearrange("p a j -> p (a j)"), func=ACT.Exp)
+        nc.vector.tensor_tensor(out=zz[:], in0=wgt[:], in1=zacc[:], op=ALU.mult)
+        nc.vector.tensor_reduce(out=zr[:], in_=zz[:].rearrange("p (a j) -> p a j", j=4), axis=AX.X, op=ALU.add)
+        nc.vector.reciprocal(out=rr[:], in_=zr[:])
+        nc.vector.tensor_tensor(
+            out=gg[:].rearrange("p (a j) -> p a j", j=4),
+            in0=wgt[:].rearrange("p (a j) -> p a j", j=4),
+            in1=rr[:].unsqueeze(2).to_broadcast([P, 8, 4]),
+            op=ALU.mult,
+        )
+        nc.vector.tensor_scalar(out=gs[:], in0=gg[:], scalar1=1e-30, scalar2=None, op0=ALU.max)
+        nc.vector.reciprocal(out=rec[:], in_=gs[:, 0:16])
+        nc.vector.scalar_tensor_tensor(
+            out=kap[:], in0=gs[:, 16:32], scalar=0.4 / 0.6, in1=rec[:], op0=ALU.mult, op1=ALU.mult
+        )
+        nc.vector.tensor_scalar(out=ff[:], in0=gg[:, 0:16], scalar1=-0.6 * V, scalar2=None, op0=ALU.mult)
+
+        acc = keep.tile([P, 16], F32, name="acc")
+        nmu = keep.tile([P, TILES], F32, name="nmu")
+        osb = [pool.tile([P, TILES, CH], F32, name="osb%d" % h, tag="wbraw", bufs=2, align_bytes=64) for h in range(HALVES)]
+        pts, xcs, ecode, escale = {}, {}, {}, {}
+
+        def ln(t):
+            for j in range(CHUNKS):
+                k = CHUNKS * t + j
+                cols = slice(CH * j, CH * (j + 1))
+                nc.scalar.activation(
+                    out=ee[t][:, cols], in_=ee[t][:, cols], func=ACT.Ln, bias=1.0, scale=kap[:, k : k + 1]
+                )
+
+        def prod(t):
+            p = pool.tile([P, V], F32, name="pt", tag="big", bufs=2, align_bytes=64)
+            pts[t] = p
+            for j in range(CHUNKS):
+                k = CHUNKS * t + j
+                cols = slice(CH * j, CH * (j + 1))
+                nc.vector.scalar_tensor_tensor(
+                    out=p[:, cols], in0=ee[t][:, cols], scalar=80.0, in1=es[t][:, cols], op0=ALU.min, op1=ALU.mult,
+                    accum_out=acc[:, k : k + 1],
+                )
+
+        def mean(t):
+            j4 = pool.tile([P, 4], F32, name="j4", tag="j4", bufs=2)
+            nc.vector.scalar_tensor_tensor(
+                out=j4[:], in0=acc[:, 4 * t : 4 * t + 4], scalar=-1.0, in1=gg[:, 4 * t : 4 * t + 4],
+                op0=ALU.mult, op1=ALU.mult, accum_out=nmu[:, t : t + 1],
+            )
+
+        def centre(t):
+            nc.vector.scalar_tensor_tensor(
+                out=pts[t][:], in0=es[t][:], scalar=nmu[:, t : t + 1], in1=pts[t][:], op0=ALU.mult, op1=ALU.add
+            )
+
+        def gain(t, j):
+            if j == 0:
+                xc = pool.tile([P, V], BF16, name="xc", tag="raw", bufs=8, align_bytes=64)
+                xcs[t] = xc
+            k = CHUNKS * t + j
+            cols = slice(CH * j, CH * (j + 1))
+            nc.vector.scalar_tensor_tensor(
+                out=xcs[t][:, cols], in0=pts[t][:, cols], scalar=ff[:, k : k + 1], in1=cb[:, cols],
+                op0=ALU.mult, op1=ALU.mult,
+            )
+
+        egrp = {}
+
+        def tr_e(t, i, n, eng):
+            words = xcs[t][:].bitcast(F32)
+            b = bank()
+            w = n * 2 * P
+            v = b[:, :w].rearrange("p (g u r) -> p g u r", g=n, u=2)
+            for gi in range(n):
+                g = i + gi
+                for u in range(2):
+                    nc.tensor.transpose(v[:, gi, u, :], words[:, 256 * g + u : 256 * (g + 1) : 2], ident[:])
+            q = pool.tile([P, 2 * P * PACK], BF16, name="egrp", tag="hgrp", bufs=3, align_bytes=64)
+            o = q[:].bitcast(F32)[:, :w].rearrange("p (g r u) -> p g r u", g=n, u=2)
+            s = b[:, :w].rearrange("p (g u r) -> p g r u", g=n, u=2)
+            if eng == "s":
+                nc.scalar.copy(out=o, in_=s)
+            else:
+                nc.vector.tensor_copy(out=o, in_=s)
+            egrp[t, i] = q
+
+        def q_e(t, i, n):
+            if t not in ecode:
+                a = pool.tile([P, VG * P], U32, name="ecode", tag="ecode", bufs=3, align_bytes=64)
+                b = pool.tile([P, VG * P], U8, name="escale", tag="escale", bufs=3, align_bytes=64)
+                ecode[t], escale[t] = a, b
+            cols = slice(P * i, P * (i + n))
+            nc.vector.quantize_mx(
+                out=ecode[t][:, cols].bitcast(FP8X4), scales=escale[t][:, cols], in_=egrp[t, i][:, : n * P * PACK]
+            )
+
+        obank = {}
+
+        def mm_o(t, h, g):
+            if g == 0:
+                obank[t, h] = bank()
+            rows = slice(P * g, P * (g + 1))
+            cols = slice(CH * h, CH * (h + 1))
+            nc.tensor.matmul_mx(
+                out=obank[t, h][:],
+                lhsT=ecode[t][:, rows].bitcast(FP8X4),
+                lhsT_scale=escale[t][:, rows],
+                rhs=bcode[g][:, cols].bitcast(FP8X4),
+                rhs_scale=bscale[g][:, cols],
+                start=(g == 0),
+                stop=(g == VG - 1),
+            )
+
+        out_view = out_0.rearrange("(p t) m -> p t m", t=TILES)
+
+        def put_o(t, h, eng):
+            if eng == "s":
+                nc.scalar.copy(out=osb[h][:, t, :], in_=obank[t, h][:])
+            else:
+                nc.vector.tensor_copy(out=osb[h][:, t, :], in_=obank[t, h][:])
+            nc.sync.dma_start(out=out_view[:, t, CH * h : CH * (h + 1)], in_=osb[h][:, t, :])
+
+        def project(t):
+            for h in range(HALVES):
+                for g in range(VG):
+                    mm_o(t, h, g)
+
+        ln(0)
+        il_b(5, "s")
+        ln(1)
+        il_b(6, "s")
+        prod(0)
+        q_b(5)
+        mean(0)
+        centre(0)
+        for j in range(CHUNKS):
+            gain(0, j)
+        tr_e(0, 0, 2, "s")
+        tr_e(0, 2, 2, "s")
+        ln(2)
+        il_b(7, "s")
+        prod(1)
+        q_b(6)
+        mean(1)
+        q_e(0, 0, 2)
+        q_e(0, 2, 2)
+        centre(1)
+        for j in range(CHUNKS):
+            gain(1, j)
+        tr_e(1, 0, 2, "s")
+        tr_e(1, 2, 2, "s")
+        ln(3)
+        q_b(7)
+        project(0)
+        prod(2)
+        q_e(1, 0, 2)
+        mean(2)
+        q_e(1, 2, 2)
+        project(1)
+        put_o(0, 0, "s")
+        put_o(0, 1, "s")
+        put_o(1, 0, "s")
+        put_o(1, 1, "s")
+        centre(2)
+        for j in range(CHUNKS):
+            gain(2, j)
+        tr_e(2, 0, 2, "s")
+        tr_e(2, 2, 2, "s")
+        prod(3)
+        q_e(2, 0, 2)
+        mean(3)
+        q_e(2, 2, 2)
+        project(2)
+        centre(3)
+        for j in range(CHUNKS):
+            gain(3, j)
+            tr_e(3, j, 1, "s")
+            if j > 0:
+                q_e(3, j - 1, 1)
+        q_e(3, CHUNKS - 1, 1)
+        put_o(2, 0, "s")
+        put_o(2, 1, "s")
+        for g in range(VG):
+            for h in range(HALVES):
+                mm_o(3, h, g)
+        put_o(3, 0, "v")
+        put_o(3, 1, "s")
+
+        fsc = keep.tile([P, O], U8, name="fsc", align_bytes=64)
+        fcode = keep.tile([P, O], U32, name="fcode", align_bytes=64)
+        fg = [pool.tile([P, CH * PACK], BF16, name="fg%d" % h, tag="grp", bufs=6, align_bytes=64) for h in range(HALVES)]
+
+        def il_f(h, lo, hi, eng):
+            d, s = views(fg[h], osb[h], lo, hi)
+            if eng == "v":
+                nc.vector.tensor_copy(out=d, in_=s)
+            else:
+                nc.scalar.copy(out=d, in_=s)
+
+        def q_f(h, lo, hi):
+            cols = slice(CH * h + lo, CH * h + hi)
+            nc.vector.quantize_mx(
+                out=fcode[:, cols].bitcast(FP8X4), scales=fsc[:, cols], in_=fg[h][:, PACK * lo : PACK * hi]
+            )
+
+        codes_view = out_1[0].rearrange("p m t -> p (m t)").bitcast(I32)
+        il_f(0, 0, 512, "v")
+        il_f(1, 256, 512, "s")
+        il_f(1, 0, 256, "v")
+        q_f(0, 0, 512)
+        nc.sync.dma_start(out=codes_view[:, 0:CH], in_=fcode[:, 0:CH].bitcast(I32))
+        q_f(1, 0, 256)
+        q_f(1, 256, 512)
+        nc.sync.dma_start(out=codes_view[:, CH:O], in_=fcode[:, CH:O].bitcast(I32))
+        for q in range(4):
+            nc.sync.dma_start(
+                out=out_2[0, 4 * q : 4 * q + 4, :].bitcast(I32), in_=fsc[32 * q : 32 * q + 4, :].bitcast(I32)
+            )

@@ -51,22 +51,19 @@ def tile_jsdlogitgradgainprojection_kernel(tc, hs, ht, ws, wt, c, wb, out_0, out
 
         raws = {}
 
-        def load_w(x, c_, g):
+        def load_w(x, c_, g, cuts=(0, CH)):
             src = ws if x == 0 else wt
             r = pool.tile([P, PACK, CH], BF16, name="raw", tag="raw", bufs=8, align_bytes=64)
-            nc.sync.dma_start(
-                out=r[:],
-                in_=src[KP * g : KP * (g + 1), CH * c_ : CH * (c_ + 1)].rearrange("(p j) w -> p j w", j=PACK),
-            )
+            rows = src[KP * g : KP * (g + 1), CH * c_ : CH * (c_ + 1)].rearrange("(p j) w -> p j w", j=PACK)
+            for lo, hi in zip(cuts[:-1], cuts[1:]):
+                nc.sync.dma_start(out=r[:, :, lo:hi], in_=rows[:, :, lo:hi])
             raws[x, c_, g] = r
 
         hraw = [pool.tile([P, TILES, D], BF16, name="hraw%d" % x, tag="big", bufs=2, align_bytes=64) for x in (0, 1)]
 
-        def load_h(x, half):
+        def load_h(x, lo, hi):
             src = (hs if x == 0 else ht).rearrange("(p t) k -> p t k", t=TILES)
-            nc.sync.dma_start(
-                out=hraw[x][:, 2 * half : 2 * half + 2, :], in_=src[:, 2 * half : 2 * half + 2, :]
-            )
+            nc.sync.dma_start(out=hraw[x][:, lo:hi, :], in_=src[:, lo:hi, :])
 
         wbraw = {}
 
@@ -93,7 +90,10 @@ def tile_jsdlogitgradgainprojection_kernel(tc, hs, ht, ws, wt, c, wb, out_0, out
                 new_grp((x, c_, g))
             d, s = views(grps[x, c_, g], raws[x, c_, g], lo, hi)
             if x == 0:
-                nc.vector.tensor_scalar(out=d, in0=s, scalar1=-1.0, scalar2=None, op0=ALU.mult)
+                if eng == "v":
+                    nc.vector.tensor_scalar(out=d, in0=s, scalar1=-1.0, scalar2=None, op0=ALU.mult)
+                else:
+                    nc.scalar.activation(out=d, in_=s, func=ACT.Copy, scale=-1.0)
             elif eng == "v":
                 nc.vector.tensor_copy(out=d, in_=s)
             else:
@@ -101,24 +101,59 @@ def tile_jsdlogitgradgainprojection_kernel(tc, hs, ht, ws, wt, c, wb, out_0, out
 
         wcode, wscale = {}, {}
 
+        def alloc_w(x, c_):
+            a = pool.tile([P, DG * CH], U32, name="wcode%d" % x, tag="wcode%d" % x, bufs=2, align_bytes=64)
+            b = pool.tile([P, DG * CH], U8, name="wscale%d" % x, tag="wscale%d" % x, bufs=2, align_bytes=64)
+            wcode[x, c_], wscale[x, c_] = a, b
+
         def q_w(x, c_, g):
             if (x, c_) not in wcode:
-                a = pool.tile([P, DG * CH], U32, name="wcode%d" % x, tag="wcode%d" % x, bufs=2, align_bytes=64)
-                b = pool.tile([P, DG * CH], U8, name="wscale%d" % x, tag="wscale%d" % x, bufs=2, align_bytes=64)
-                wcode[x, c_], wscale[x, c_] = a, b
+                alloc_w(x, c_)
             cols = slice(CH * g, CH * (g + 1))
             nc.vector.quantize_mx(
                 out=wcode[x, c_][:, cols].bitcast(FP8X4), scales=wscale[x, c_][:, cols], in_=grps[x, c_, g][:]
             )
 
+        GP = 128
+        gtile = {}
+
+        def g_piece(key, src, i):
+            q = pool.tile([P, GP * PACK], BF16, name="gpiece", tag="gpiece", bufs=1, align_bytes=64)
+            gtile[key] = q
+            d = q[:].rearrange("p (c i t) -> p c t i", i=4, t=PACK)
+            s = src[:, :, GP * i : GP * (i + 1)].rearrange("p t (c i) -> p c t i", i=4)
+            nc.gpsimd.tensor_scalar(out=d, in0=s, scalar1=1.0, scalar2=0.0, op0=ALU.mult, op1=ALU.add)
+
+        def g_w(c_, i):
+            g_piece((c_, i), raws[1, c_, 1], i)
+
+        def gq_w(c_, i):
+            if (1, c_) not in wcode:
+                alloc_w(1, c_)
+            cols = slice(CH + GP * i, CH + GP * (i + 1))
+            nc.vector.quantize_mx(
+                out=wcode[1, c_][:, cols].bitcast(FP8X4), scales=wscale[1, c_][:, cols], in_=gtile[c_, i][:]
+            )
+
+        def g_b(b_, i):
+            g, h = b_ // 2, b_ % 2
+            g_piece(("b", b_, i), wbraw[g][:, :, CH * h : CH * (h + 1)], i)
+
+        def gq_b(b_, i):
+            g, h = b_ // 2, b_ % 2
+            cols = slice(CH * h + GP * i, CH * h + GP * (i + 1))
+            nc.vector.quantize_mx(
+                out=bcode[g][:, cols].bitcast(FP8X4), scales=bscale[g][:, cols], in_=gtile["b", b_, i][:]
+            )
+
         bcode = [keep.tile([P, O], U32, name="bcode%d" % g, align_bytes=64) for g in range(VG)]
         bscale = [keep.tile([P, O], U8, name="bscale%d" % g, align_bytes=64) for g in range(VG)]
 
-        def il_b(i, eng):
+        def il_b(i, eng, lo=0, hi=CH):
             g, h = i // 2, i % 2
-            new_grp(("b", i))
-            d = grps["b", i][:].rearrange("p (c i t) -> p c t i", i=4, t=PACK)
-            s = wbraw[g][:, :, CH * h : CH * (h + 1)].rearrange("p t (c i) -> p c t i", i=4)
+            if ("b", i) not in grps:
+                new_grp(("b", i))
+            d, s = views(grps["b", i], wbraw[g][:, :, CH * h : CH * (h + 1)], lo, hi)
             if eng == "v":
                 nc.vector.tensor_copy(out=d, in_=s)
             else:
@@ -166,121 +201,162 @@ def tile_jsdlogitgradgainprojection_kernel(tc, hs, ht, ws, wt, c, wb, out_0, out
 
         units = {}
 
-        def unit_pe(t, j):
-            bn, bt, bd = bank(), bank(), bank()
-            for b, x in ((bn, 0), (bt, 1)):
-                for g in range(DG):
-                    mm_h(b, x, t, j, g, g == 0, g == DG - 1)
-            order = [(0, 0), (0, 1), (1, 0), (1, 1)]
-            for i, (x, g) in enumerate(order):
-                mm_h(bd, x, t, j, g, i == 0, i == 3)
-            units[t, j] = (bn, bt, bd)
+        def pe_n(t, j):
+            b = bank()
+            for g in range(DG):
+                mm_h(b, 0, t, j, g, g == 0, g == DG - 1)
+            units["n", t, j] = b
 
-        def unit_max(t, j):
-            bn, bt, bd = units[t, j]
+        def pe_t(t, j):
+            b = bank()
+            for g in range(DG):
+                mm_h(b, 1, t, j, g, g == 0, g == DG - 1)
+            units["t", t, j] = b
+            b = bank()
+            for i, (x, g) in enumerate([(0, 0), (0, 1), (1, 0), (1, 1)]):
+                mm_h(b, x, t, j, g, i == 0, i == 3)
+            units["d", t, j] = b
+
+        def min_n(t, j):
             k = CHUNKS * t + j
-            nc.vector.tensor_reduce(out=nmx[:, k : k + 1], in_=bn[:], axis=AX.X, op=ALU.min)
-            nc.vector.tensor_reduce(out=nmx[:, 16 + k : 17 + k], in_=bt[:], axis=AX.X, op=ALU.max, negate=True)
+            nc.vector.tensor_reduce(out=nmx[:, k : k + 1], in_=units["n", t, j][:], axis=AX.X, op=ALU.min)
+
+        def max_t(t, j):
+            k = CHUNKS * t + j
+            nc.vector.tensor_reduce(
+                out=nmx[:, 16 + k : 17 + k], in_=units["t", t, j][:], axis=AX.X, op=ALU.max, negate=True
+            )
+
+        def ebias_td(t, j):
+            k = CHUNKS * t + j
             nc.gpsimd.tensor_tensor(
                 out=ebias[:, k : k + 1], in0=nmx[:, 16 + k : 17 + k], in1=nmx[:, k : k + 1], op=ALU.subtract
             )
 
-        def unit_exp(t, j):
-            bn, bt, bd = units[t, j]
+        def exp_n(t, j):
             k = CHUNKS * t + j
             cols = slice(CH * j, CH * (j + 1))
             nc.scalar.activation(
-                out=es[t][:, cols], in_=bn[:], func=ACT.Exp, bias=nmx[:, k : k + 1], scale=-1.0,
+                out=es[t][:, cols], in_=units["n", t, j][:], func=ACT.Exp, bias=nmx[:, k : k + 1], scale=-1.0,
                 accum_out=zacc[:, k : k + 1],
             )
-            junk = pool.tile([P, CH], F32, name="junk", tag="junk", bufs=2)
+
+        def exp_t(t, j):
+            k = CHUNKS * t + j
+            cols = slice(CH * j, CH * (j + 1))
             nc.scalar.activation(
-                out=junk[:], in_=bt[:], func=ACT.Exp, bias=nmx[:, 16 + k : 17 + k], scale=1.0,
+                out=ee[t][:, cols], in_=units["t", t, j][:], func=ACT.Exp, bias=nmx[:, 16 + k : 17 + k], scale=1.0,
                 accum_out=zacc[:, 16 + k : 17 + k],
             )
 
-        def unit_ratio(t, j):
-            bn, bt, bd = units[t, j]
+        def exp_d(t, j):
             k = CHUNKS * t + j
             cols = slice(CH * j, CH * (j + 1))
-            nc.scalar.activation(out=ee[t][:, cols], in_=bd[:], func=ACT.Exp, bias=ebias[:, k : k + 1], scale=1.0)
+            nc.scalar.activation(
+                out=ee[t][:, cols], in_=units["d", t, j][:], func=ACT.Exp, bias=ebias[:, k : k + 1], scale=1.0
+            )
 
-        load_w(0, 0, 0)
+        load_w(0, 0, 0, (0, 256, 512))
         load_w(0, 0, 1)
-        load_h(0, 0)
+        load_h(0, 0, 1)
         load_w(1, 0, 0)
+        load_h(1, 0, 1)
         load_w(1, 0, 1)
-        load_h(1, 0)
-        load_h(0, 1)
-        load_h(1, 1)
-        for x in (0, 1):
-            for g in (0, 1):
-                load_w(x, 1, g)
-        load_wb(0)
+        load_h(0, 1, 2)
+        load_h(1, 1, 2)
+        load_w(0, 1, 0)
+        load_h(0, 2, 4)
+        load_h(1, 2, 4)
+        load_w(0, 1, 1)
+        load_w(1, 1, 0)
+        load_w(1, 1, 1)
 
-        il_w(0, 0, 0, "v")
-        il_w(0, 0, 1, "v")
+        il_w(0, 0, 0, "v", 0, 256)
+        il_w(0, 0, 0, "v", 256, 416)
+        il_w(0, 0, 0, "s", 416, 512)
+        il_w(0, 0, 1, "s", 320, 512)
         q_w(0, 0, 0)
-        q_w(0, 0, 1)
+        il_w(0, 0, 1, "v", 0, 320)
         tr_h(0, 0)
-        il_w(1, 0, 0, "s")
-        il_w(1, 0, 1, "v")
-        tr_h(1, 0)
+        il_w(1, 0, 0, "s", 320, 512)
+        il_w(1, 0, 0, "v", 0, 320)
+        q_w(0, 0, 1)
         q_h(0, 0)
+        tr_h(1, 0)
+        pe_n(0, 0)
+        q_w(1, 0, 0)
+        min_n(0, 0)
+        il_w(1, 0, 1, "v", 0, 320)
+        il_w(1, 0, 1, "s", 320, 512)
+        exp_n(0, 0)
         q_h(1, 0)
         q_w(1, 0, 1)
-        q_w(1, 0, 0)
         tr_h(0, 1)
         tr_h(1, 1)
-        il_w(0, 1, 0, "v")
         q_h(0, 1)
-        q_h(1, 1)
 
-        vfill = {}
-        sfill = {}
+        vfill, sfill, gfill = {}, {}, {}
         for j in range(CHUNKS):
             for t in range(TILES):
                 vfill[j, t] = []
                 sfill[j, t] = []
-        vfill[0, 0] += [lambda: q_h(0, 2), lambda: q_h(1, 2)]
-        vfill[0, 1] += [lambda: q_h(0, 3), lambda: q_h(1, 3)]
-        sfill[0, 0] += [lambda: tr_h(0, 2), lambda: tr_h(1, 2), lambda: tr_h(0, 3), lambda: tr_h(1, 3),
-                        lambda: il_w(1, 1, 0, "s")]
-        for j in range(CHUNKS - 1):
-            n = j + 1
-            vfill[j, 0].append(lambda n=n: il_w(0, n, 1, "v"))
-            vfill[j, 1] += [lambda n=n: q_w(0, n, 0), lambda n=n: q_w(1, n, 0)]
-            vfill[j, 2] += [lambda n=n: q_w(0, n, 1), lambda n=n: q_w(1, n, 1)]
-            sfill[j, 0].append(lambda n=n: il_w(1, n, 1, "s", 0, 256))
-            vfill[j, 1].append(lambda n=n: il_w(1, n, 1, "v", 256, 512))
-            if n + 1 < CHUNKS:
-                vfill[j, 3].append(lambda n=n: il_w(0, n + 1, 0, "v"))
-                sfill[j, 3].append(lambda n=n: il_w(1, n + 1, 0, "s"))
-        vfill[2, 2].append(lambda: il_b(0, "v"))
-        vfill[2, 3] += [lambda: q_b(0), lambda: il_b(1, "v")]
-        vfill[3, 0] += [lambda: q_b(1), lambda: il_b(2, "v")]
-        vfill[3, 1] += [lambda: q_b(2), lambda: il_b(3, "v")]
-        sfill[3, 1].append(lambda: il_b(4, "s"))
-        vfill[3, 2] += [lambda: q_b(3)]
+                gfill[j, t] = []
+        vfill[0, 0] += [lambda: q_h(1, 1), lambda: il_w(0, 1, 0, "v")]
+        vfill[0, 1] += [lambda: q_w(0, 1, 0), lambda: q_h(0, 2), lambda: q_h(1, 2), lambda: il_w(0, 1, 1, "v")]
+        sfill[0, 1] += [lambda: tr_h(0, 2), lambda: tr_h(1, 2), lambda: tr_h(0, 3), lambda: tr_h(1, 3)]
+        vfill[0, 2] += [lambda: q_h(0, 3), lambda: q_h(1, 3)]
+        sfill[0, 1] += [lambda: il_w(1, 1, 0, "s")]
+        vfill[0, 2] += [lambda: il_w(1, 1, 1, "v", 0, 384), lambda: q_w(1, 1, 0)]
+        sfill[0, 2] += [lambda: il_w(1, 1, 1, "s", 384, 512)]
+        vfill[0, 3] += [lambda: q_w(0, 1, 1), lambda: q_w(1, 1, 1)]
+        for n in (2, 3):
+            slots = [(n - 2, 3), (n - 1, 0), (n - 1, 1), (n - 1, 2)]
+            for i, sl in enumerate(slots):
+                gfill[sl].append(lambda n=n, i=i: g_w(n, i))
+            vfill[slots[0]].append(lambda n=n: il_w(0, n, 0, "v"))
+            vfill[slots[1]].append(lambda n=n: il_w(0, n, 1, "v"))
+            vfill[slots[2]] += [lambda n=n: q_w(0, n, 0), lambda n=n: q_w(1, n, 0)]
+            vfill[slots[3]] += [lambda n=n: q_w(0, n, 1)]
+            sfill[slots[0]].append(lambda n=n: il_w(1, n, 0, "s", 0, 256))
+            sfill[slots[1]].append(lambda n=n: il_w(1, n, 0, "s", 256, 512))
+            for i, sl in enumerate(slots):
+                vfill[sl].append(lambda n=n, i=i: gq_w(n, i))
+        vfill[2, 3] += [lambda: il_b(0, "v")]
+        vfill[3, 0] += [lambda: q_b(0)]
+        for i in range(4):
+            gfill[3, i].append(lambda i=i: g_b(3, i))
+            vfill[3, i].append(lambda i=i: gq_b(3, i))
 
         for j in range(CHUNKS):
             for t in range(TILES):
-                unit_pe(t, j)
-                unit_max(t, j)
-                unit_exp(t, j)
+                if (t, j) != (0, 0):
+                    pe_n(t, j)
+                    pe_t(t, j)
+                    for f in gfill[j, t]:
+                        f()
+                    min_n(t, j)
+                else:
+                    pe_t(t, j)
+                max_t(t, j)
+                ebias_td(t, j)
+                if (t, j) != (0, 0):
+                    exp_n(t, j)
+                exp_t(t, j)
                 for f in sfill[j, t]:
                     f()
-                unit_ratio(t, j)
+                if (j, t) == (CHUNKS - 1, TILES - 1):
+                    break
+                exp_d(t, j)
                 for f in vfill[j, t]:
                     f()
                 if t == 1 and j < 2:
-                    for g in (0, 1):
-                        for x in (0, 1):
-                            load_w(x, j + 2, g)
-                    load_wb(j + 1)
-                    if j == 0:
-                        nc.sync.dma_start(out=cb[:], in_=c.partition_broadcast(P))
-                if t == 3 and j == 2:
+                    for x, g in ((1, 1), (0, 0), (1, 0), (0, 1)):
+                        load_w(x, j + 2, g)
+                    load_wb(j)
+                if (j, t) == (2, 0):
+                    nc.sync.dma_start(out=cb[:], in_=c.partition_broadcast(P))
+                if t == 2 and j == 3:
+                    load_wb(2)
                     load_wb(3)
 
         stat = keep.tile([P, 8, 4], F32, name="stat")
@@ -296,12 +372,17 @@ def tile_jsdlogitgradgainprojection_kernel(tc, hs, ht, ws, wt, c, wb, out_0, out
         ff = keep.tile([P, 16], F32, name="ff")
         nmx3 = nmx[:].rearrange("p (a j) -> p a j", j=4)
         nc.vector.tensor_reduce(out=nm[:], in_=nmx3, axis=AX.X, op=ALU.min)
-        q_b(4)
+        gq_b(3, 3)
         nc.vector.tensor_tensor(out=stat[:], in0=nm[:].unsqueeze(2).to_broadcast([P, 8, 4]), in1=nmx3, op=ALU.subtract)
         nc.scalar.activation(out=wgt[:], in_=stat[:].rearrange("p a j -> p (a j)"), func=ACT.Exp)
+        exp_d(TILES - 1, CHUNKS - 1)
+        il_b(1, "v", 0, 128)
         nc.vector.tensor_tensor(out=zz[:], in0=wgt[:], in1=zacc[:], op=ALU.mult)
+        il_b(1, "v", 128, 256)
         nc.vector.tensor_reduce(out=zr[:], in_=zz[:].rearrange("p (a j) -> p a j", j=4), axis=AX.X, op=ALU.add)
+        il_b(1, "v", 256, 384)
         nc.vector.reciprocal(out=rr[:], in_=zr[:])
+        il_b(1, "v", 384, 512)
         nc.vector.tensor_tensor(
             out=gg[:].rearrange("p (a j) -> p a j", j=4),
             in0=wgt[:].rearrange("p (a j) -> p a j", j=4),
@@ -314,7 +395,6 @@ def tile_jsdlogitgradgainprojection_kernel(tc, hs, ht, ws, wt, c, wb, out_0, out
             out=kap[:], in0=gs[:, 16:32], scalar=0.4 / 0.6, in1=rec[:], op0=ALU.mult, op1=ALU.mult
         )
         nc.vector.tensor_scalar(out=ff[:], in0=gg[:, 0:16], scalar1=-0.6 * V, scalar2=None, op0=ALU.mult)
-
         acc = keep.tile([P, 16], F32, name="acc")
         nmu = keep.tile([P, TILES], F32, name="nmu")
         osb = [pool.tile([P, TILES, CH], F32, name="osb%d" % h, tag="wbraw", bufs=2, align_bytes=64) for h in range(HALVES)]
@@ -347,9 +427,12 @@ def tile_jsdlogitgradgainprojection_kernel(tc, hs, ht, ws, wt, c, wb, out_0, out
             )
 
         def centre(t):
-            nc.vector.scalar_tensor_tensor(
-                out=pts[t][:], in0=es[t][:], scalar=nmu[:, t : t + 1], in1=pts[t][:], op0=ALU.mult, op1=ALU.add
-            )
+            for i in (0, 1):
+                cols = slice(1024 * i, 1024 * (i + 1))
+                nc.vector.scalar_tensor_tensor(
+                    out=pts[t][:, cols], in0=es[t][:, cols], scalar=nmu[:, t : t + 1], in1=pts[t][:, cols],
+                    op0=ALU.mult, op1=ALU.add,
+                )
 
         def gain(t, j):
             if j == 0:
@@ -424,21 +507,23 @@ def tile_jsdlogitgradgainprojection_kernel(tc, hs, ht, ws, wt, c, wb, out_0, out
                     mm_o(t, h, g)
 
         ln(0)
-        il_b(5, "s")
+        il_b(2, "s")
         ln(1)
-        il_b(6, "s")
+        il_b(4, "s")
+        q_b(1)
         prod(0)
-        q_b(5)
         mean(0)
         centre(0)
         for j in range(CHUNKS):
             gain(0, j)
         tr_e(0, 0, 2, "s")
         tr_e(0, 2, 2, "s")
+        il_b(5, "s")
         ln(2)
-        il_b(7, "s")
+        il_b(6, "s")
+        q_b(2)
         prod(1)
-        q_b(6)
+        q_b(4)
         mean(1)
         q_e(0, 0, 2)
         q_e(0, 2, 2)
@@ -447,53 +532,35 @@ def tile_jsdlogitgradgainprojection_kernel(tc, hs, ht, ws, wt, c, wb, out_0, out
             gain(1, j)
         tr_e(1, 0, 2, "s")
         tr_e(1, 2, 2, "s")
+        il_b(7, "s")
         ln(3)
+        prod(2)
+        q_b(5)
+        q_b(6)
+        mean(2)
+        q_e(1, 0, 2)
+        q_e(1, 2, 2)
+        centre(2)
         q_b(7)
         project(0)
-        prod(2)
-        q_e(1, 0, 2)
-        mean(2)
-        q_e(1, 2, 2)
-        project(1)
         put_o(0, 0, "s")
         put_o(0, 1, "s")
-        put_o(1, 0, "s")
-        put_o(1, 1, "s")
-        centre(2)
         for j in range(CHUNKS):
             gain(2, j)
         tr_e(2, 0, 2, "s")
         tr_e(2, 2, 2, "s")
+        project(1)
+        put_o(1, 0, "s")
+        put_o(1, 1, "s")
         prod(3)
         q_e(2, 0, 2)
         mean(3)
         q_e(2, 2, 2)
         project(2)
         centre(3)
-        for j in range(CHUNKS):
-            gain(3, j)
-            tr_e(3, j, 1, "s")
-            if j > 0:
-                q_e(3, j - 1, 1)
-        q_e(3, CHUNKS - 1, 1)
-        put_o(2, 0, "s")
-        put_o(2, 1, "s")
-        for g in range(VG):
-            for h in range(HALVES):
-                mm_o(3, h, g)
-        put_o(3, 0, "v")
-        put_o(3, 1, "s")
-
         fsc = keep.tile([P, O], U8, name="fsc", align_bytes=64)
         fcode = keep.tile([P, O], U32, name="fcode", align_bytes=64)
         fg = [pool.tile([P, CH * PACK], BF16, name="fg%d" % h, tag="grp", bufs=6, align_bytes=64) for h in range(HALVES)]
-
-        def il_f(h, lo, hi, eng):
-            d, s = views(fg[h], osb[h], lo, hi)
-            if eng == "v":
-                nc.vector.tensor_copy(out=d, in_=s)
-            else:
-                nc.scalar.copy(out=d, in_=s)
 
         def q_f(h, lo, hi):
             cols = slice(CH * h + lo, CH * h + hi)
@@ -501,15 +568,44 @@ def tile_jsdlogitgradgainprojection_kernel(tc, hs, ht, ws, wt, c, wb, out_0, out
                 out=fcode[:, cols].bitcast(FP8X4), scales=fsc[:, cols], in_=fg[h][:, PACK * lo : PACK * hi]
             )
 
+        def pre(h, lo, hi, eng):
+            d, s = views(fg[h], osb[h], lo, hi)
+            if eng == "v":
+                nc.vector.tensor_copy(out=d[:, :, 0:3, :], in_=s[:, :, 0:3, :])
+            else:
+                nc.scalar.copy(out=d[:, :, 0:3, :], in_=s[:, :, 0:3, :])
+
+        def last(h, eng):
+            d = fg[h][:].rearrange("p (m t) -> p m t", t=PACK)[:, :, 3]
+            if eng == "v":
+                nc.vector.tensor_copy(out=d, in_=obank[3, h][:])
+            else:
+                nc.scalar.copy(out=d, in_=obank[3, h][:])
+
         codes_view = out_1[0].rearrange("p m t -> p (m t)").bitcast(I32)
-        il_f(0, 0, 512, "v")
-        il_f(1, 256, 512, "s")
-        il_f(1, 0, 256, "v")
+        put_o(2, 0, "s")
+        put_o(2, 1, "s")
+        for j in range(CHUNKS):
+            gain(3, j)
+            tr_e(3, j, 1, "s")
+            if j > 0:
+                q_e(3, j - 1, 1)
+        pre(0, 0, 256, "v")
+        q_e(3, CHUNKS - 1, 1)
+        pre(0, 256, 512, "v")
+        pre(1, 0, 256, "s")
+        pre(1, 256, 512, "s")
+        for g in range(VG):
+            for h in range(HALVES):
+                mm_o(3, h, g)
+        last(0, "v")
+        last(1, "s")
         q_f(0, 0, 512)
         nc.sync.dma_start(out=codes_view[:, 0:CH], in_=fcode[:, 0:CH].bitcast(I32))
-        q_f(1, 0, 256)
-        q_f(1, 256, 512)
+        q_f(1, 0, 512)
         nc.sync.dma_start(out=codes_view[:, CH:O], in_=fcode[:, CH:O].bitcast(I32))
+        put_o(3, 0, "s")
+        put_o(3, 1, "s")
         for q in range(4):
             nc.sync.dma_start(
                 out=out_2[0, 4 * q : 4 * q + 4, :].bitcast(I32), in_=fsc[32 * q : 32 * q + 4, :].bitcast(I32)

@@ -120,8 +120,8 @@ def tile_jsdlogitgradgainprojection_kernel(tc, hs, ht, ws, wt, c, wb, out_0, out
         def g_piece(key, src, i):
             q = pool.tile([P, GP * PACK], BF16, name="gpiece", tag="gpiece", bufs=1, align_bytes=64)
             gtile[key] = q
-            d = q[:].rearrange("p (c i t) -> p c t i", i=4, t=PACK)
-            s = src[:, :, GP * i : GP * (i + 1)].rearrange("p t (c i) -> p c t i", i=4)
+            d = q[:].rearrange("p (c t) -> p c t", t=PACK)
+            s = src[:, :, GP * i : GP * (i + 1)].rearrange("p t c -> p c t")
             nc.gpsimd.tensor_scalar(out=d, in0=s, scalar1=1.0, scalar2=0.0, op0=ALU.mult, op1=ALU.add)
 
         def g_w(c_, i):
@@ -265,9 +265,11 @@ def tile_jsdlogitgradgainprojection_kernel(tc, hs, ht, ws, wt, c, wb, out_0, out
         load_h(0, 1, 2)
         load_h(1, 1, 2)
         load_w(0, 1, 0)
-        load_h(0, 2, 4)
-        load_h(1, 2, 4)
+        load_h(0, 2, 3)
+        load_h(1, 2, 3)
         load_w(0, 1, 1)
+        load_h(0, 3, 4)
+        load_h(1, 3, 4)
         load_w(1, 1, 0)
         load_w(1, 1, 1)
 
@@ -317,8 +319,9 @@ def tile_jsdlogitgradgainprojection_kernel(tc, hs, ht, ws, wt, c, wb, out_0, out
             vfill[slots[1]].append(lambda n=n: il_w(0, n, 1, "v"))
             vfill[slots[2]] += [lambda n=n: q_w(0, n, 0), lambda n=n: q_w(1, n, 0)]
             vfill[slots[3]] += [lambda n=n: q_w(0, n, 1)]
-            sfill[slots[0]].append(lambda n=n: il_w(1, n, 0, "s", 0, 256))
-            sfill[slots[1]].append(lambda n=n: il_w(1, n, 0, "s", 256, 512))
+            sfill[slots[0]].append(lambda n=n: il_w(1, n, 0, "s", 0, 224))
+            sfill[slots[1]].append(lambda n=n: il_w(1, n, 0, "s", 224, 448))
+            vfill[slots[2]].insert(0, lambda n=n: il_w(1, n, 0, "v", 448, 512))
             for i, sl in enumerate(slots):
                 vfill[sl].append(lambda n=n, i=i: gq_w(n, i))
         vfill[2, 3] += [lambda: il_b(0, "v")]

@@ -229,8 +229,9 @@ def tile_jsdlogitgradgainprojection_kernel(tc, hs, ht, ws, wt, c, wb, out_0, out
 
         def ebias_td(t, j):
             k = CHUNKS * t + j
-            nc.gpsimd.tensor_tensor(
-                out=ebias[:, k : k + 1], in0=nmx[:, 16 + k : 17 + k], in1=nmx[:, k : k + 1], op=ALU.subtract
+            nc.scalar.activation(
+                out=ebias[:, k : k + 1], in_=nmx[:, k : k + 1], func=ACT.Identity, scale=-1.0,
+                bias=nmx[:, 16 + k : 17 + k],
             )
 
         def exp_n(t, j):
@@ -243,9 +244,9 @@ def tile_jsdlogitgradgainprojection_kernel(tc, hs, ht, ws, wt, c, wb, out_0, out
 
         def exp_t(t, j):
             k = CHUNKS * t + j
-            cols = slice(CH * j, CH * (j + 1))
+            junk = pool.tile([P, CH], F32, name="junk", tag="junk", bufs=2)
             nc.scalar.activation(
-                out=ee[t][:, cols], in_=units["t", t, j][:], func=ACT.Exp, bias=nmx[:, 16 + k : 17 + k], scale=1.0,
+                out=junk[:], in_=units["t", t, j][:], func=ACT.Exp, bias=nmx[:, 16 + k : 17 + k], scale=1.0,
                 accum_out=zacc[:, 16 + k : 17 + k],
             )
 
@@ -287,8 +288,8 @@ def tile_jsdlogitgradgainprojection_kernel(tc, hs, ht, ws, wt, c, wb, out_0, out
         tr_h(1, 0)
         pe_n(0, 0)
         q_w(1, 0, 0)
-        min_n(0, 0)
         il_w(1, 0, 1, "v", 0, 320)
+        min_n(0, 0)
         il_w(1, 0, 1, "s", 320, 512)
         exp_n(0, 0)
         q_h(1, 0)
@@ -304,10 +305,11 @@ def tile_jsdlogitgradgainprojection_kernel(tc, hs, ht, ws, wt, c, wb, out_0, out
                 sfill[j, t] = []
                 gfill[j, t] = []
         vfill[0, 0] += [lambda: q_h(1, 1), lambda: il_w(0, 1, 0, "v")]
-        vfill[0, 1] += [lambda: q_w(0, 1, 0), lambda: q_h(0, 2), lambda: q_h(1, 2), lambda: il_w(0, 1, 1, "v")]
-        sfill[0, 1] += [lambda: tr_h(0, 2), lambda: tr_h(1, 2), lambda: tr_h(0, 3), lambda: tr_h(1, 3)]
+        vfill[0, 1] += [lambda: q_w(0, 1, 0), lambda: q_h(0, 2), lambda: q_h(1, 2), lambda: il_w(0, 1, 1, "v"),
+                        lambda: il_w(1, 1, 0, "v", 0, 128)]
+        sfill[0, 1] += [lambda: tr_h(0, 3), lambda: tr_h(1, 3)]
         vfill[0, 2] += [lambda: q_h(0, 3), lambda: q_h(1, 3)]
-        sfill[0, 1] += [lambda: il_w(1, 1, 0, "s")]
+        sfill[0, 1] += [lambda: il_w(1, 1, 0, "s", 128, 512)]
         vfill[0, 2] += [lambda: il_w(1, 1, 1, "v", 0, 384), lambda: q_w(1, 1, 0)]
         sfill[0, 2] += [lambda: il_w(1, 1, 1, "s", 384, 512)]
         vfill[0, 3] += [lambda: q_w(0, 1, 1), lambda: q_w(1, 1, 1)]
@@ -341,26 +343,43 @@ def tile_jsdlogitgradgainprojection_kernel(tc, hs, ht, ws, wt, c, wb, out_0, out
                 else:
                     pe_t(t, j)
                 max_t(t, j)
-                ebias_td(t, j)
                 if (t, j) != (0, 0):
                     exp_n(t, j)
+                ebias_td(t, j)
+                if (j, t) == (0, 1):
+                    tr_h(0, 2)
+                    tr_h(1, 2)
                 exp_t(t, j)
-                for f in sfill[j, t]:
-                    f()
                 if (j, t) == (CHUNKS - 1, TILES - 1):
                     break
                 exp_d(t, j)
+                for f in sfill[j, t]:
+                    f()
                 for f in vfill[j, t]:
                     f()
                 if t == 1 and j < 2:
                     for x, g in ((1, 1), (0, 0), (1, 0), (0, 1)):
                         load_w(x, j + 2, g)
-                    load_wb(j)
+                if (j, t) == (1, 2):
+                    load_wb(0)
+                if (j, t) == (2, 1):
+                    load_wb(1)
                 if (j, t) == (2, 0):
                     nc.sync.dma_start(out=cb[:], in_=c.partition_broadcast(P))
                 if t == 2 and j == 3:
                     load_wb(2)
                     load_wb(3)
+
+        escs = {}
+
+        def es_gain(i):
+            e = pool.tile([P, V // 2], F32, name="esc%d" % i, tag="raw", bufs=8, align_bytes=64)
+            escs[i] = e
+            for h in range(2):
+                cols = slice(CH * (2 * i + h), CH * (2 * i + h + 1))
+                nc.vector.tensor_tensor(
+                    out=e[:, CH * h : CH * (h + 1)], in0=es[3][:, cols], in1=cb[:, cols], op=ALU.mult
+                )
 
         stat = keep.tile([P, 8, 4], F32, name="stat")
         nm = keep.tile([P, 8], F32, name="nm")
@@ -427,6 +446,31 @@ def tile_jsdlogitgradgainprojection_kernel(tc, hs, ht, ws, wt, c, wb, out_0, out
             nc.vector.scalar_tensor_tensor(
                 out=j4[:], in0=acc[:, 4 * t : 4 * t + 4], scalar=-1.0, in1=gg[:, 4 * t : 4 * t + 4],
                 op0=ALU.mult, op1=ALU.mult, accum_out=nmu[:, t : t + 1],
+            )
+
+        nmf = keep.tile([P, 4], F32, name="nmf")
+
+        def shift3():
+            nc.vector.tensor_scalar(
+                out=nmf[:], in0=ff[:, 12:16], scalar1=nmu[:, 3:4], scalar2=None, op0=ALU.mult
+            )
+
+        def scale3():
+            for j in range(CHUNKS):
+                cols = slice(CH * j, CH * (j + 1))
+                nc.scalar.activation(
+                    out=ee[3][:, cols], in_=ee[3][:, cols], func=ACT.Identity, scale=ff[:, 12 + j : 13 + j],
+                    bias=nmf[:, j : j + 1],
+                )
+
+        def gain3(j):
+            if j == 0:
+                xc = pool.tile([P, V], BF16, name="xc", tag="raw", bufs=8, align_bytes=64)
+                xcs[3] = xc
+            cols = slice(CH * j, CH * (j + 1))
+            nc.vector.scalar_tensor_tensor(
+                out=xcs[3][:, cols], in0=ee[3][:, cols], scalar=-1e30, in1=escs[j // 2][:, CH * (j % 2) : CH * (j % 2 + 1)],
+                op0=ALU.max, op1=ALU.mult,
             )
 
         def centre(t):
@@ -497,12 +541,20 @@ def tile_jsdlogitgradgainprojection_kernel(tc, hs, ht, ws, wt, c, wb, out_0, out
 
         out_view = out_0.rearrange("(p t) m -> p t m", t=TILES)
 
+        def store_o(t, h):
+            nc.sync.dma_start(out=out_view[:, t, CH * h : CH * (h + 1)], in_=osb[h][:, t, :])
+
         def put_o(t, h, eng):
             if eng == "s":
                 nc.scalar.copy(out=osb[h][:, t, :], in_=obank[t, h][:])
             else:
                 nc.vector.tensor_copy(out=osb[h][:, t, :], in_=obank[t, h][:])
-            nc.sync.dma_start(out=out_view[:, t, CH * h : CH * (h + 1)], in_=osb[h][:, t, :])
+            if t < TILES - 1:
+                store_o(t, h)
+
+        def project_h(t, h):
+            for g in range(VG):
+                mm_o(t, h, g)
 
         def project(t):
             for h in range(HALVES):
@@ -521,9 +573,9 @@ def tile_jsdlogitgradgainprojection_kernel(tc, hs, ht, ws, wt, c, wb, out_0, out
             gain(0, j)
         tr_e(0, 0, 2, "s")
         tr_e(0, 2, 2, "s")
-        il_b(5, "s")
-        ln(2)
         il_b(6, "s")
+        ln(2)
+        il_b(5, "s")
         q_b(2)
         prod(1)
         q_b(4)
@@ -531,35 +583,37 @@ def tile_jsdlogitgradgainprojection_kernel(tc, hs, ht, ws, wt, c, wb, out_0, out
         q_e(0, 0, 2)
         q_e(0, 2, 2)
         centre(1)
+        q_b(6)
+        project_h(0, 0)
         for j in range(CHUNKS):
             gain(1, j)
         tr_e(1, 0, 2, "s")
         tr_e(1, 2, 2, "s")
+        put_o(0, 0, "s")
         il_b(7, "s")
         ln(3)
         prod(2)
         q_b(5)
-        q_b(6)
         mean(2)
         q_e(1, 0, 2)
         q_e(1, 2, 2)
+        project_h(1, 0)
         centre(2)
         q_b(7)
-        project(0)
-        put_o(0, 0, "s")
+        project_h(0, 1)
+        put_o(1, 0, "s")
         put_o(0, 1, "s")
         for j in range(CHUNKS):
             gain(2, j)
         tr_e(2, 0, 2, "s")
         tr_e(2, 2, 2, "s")
-        project(1)
-        put_o(1, 0, "s")
+        project_h(1, 1)
         put_o(1, 1, "s")
         prod(3)
         q_e(2, 0, 2)
         mean(3)
         q_e(2, 2, 2)
-        project(2)
+        project_h(2, 0)
         centre(3)
         fsc = keep.tile([P, O], U8, name="fsc", align_bytes=64)
         fcode = keep.tile([P, O], U32, name="fcode", align_bytes=64)
@@ -571,21 +625,19 @@ def tile_jsdlogitgradgainprojection_kernel(tc, hs, ht, ws, wt, c, wb, out_0, out
                 out=fcode[:, cols].bitcast(FP8X4), scales=fsc[:, cols], in_=fg[h][:, PACK * lo : PACK * hi]
             )
 
-        def pre(h, lo, hi, eng):
+        def il_f(h, lo, hi, eng):
             d, s = views(fg[h], osb[h], lo, hi)
             if eng == "v":
-                nc.vector.tensor_copy(out=d[:, :, 0:3, :], in_=s[:, :, 0:3, :])
+                nc.vector.tensor_copy(out=d, in_=s)
             else:
-                nc.scalar.copy(out=d[:, :, 0:3, :], in_=s[:, :, 0:3, :])
-
-        def last(h, eng):
-            d = fg[h][:].rearrange("p (m t) -> p m t", t=PACK)[:, :, 3]
-            if eng == "v":
-                nc.vector.tensor_copy(out=d, in_=obank[3, h][:])
-            else:
-                nc.scalar.copy(out=d, in_=obank[3, h][:])
+                nc.scalar.copy(out=d, in_=s)
 
         codes_view = out_1[0].rearrange("p m t -> p (m t)").bitcast(I32)
+
+        def put_codes(lo, hi):
+            nc.sync.dma_start(out=codes_view[:, lo:hi], in_=fcode[:, lo:hi].bitcast(I32))
+
+        project_h(2, 1)
         put_o(2, 0, "s")
         put_o(2, 1, "s")
         for j in range(CHUNKS):
@@ -593,22 +645,29 @@ def tile_jsdlogitgradgainprojection_kernel(tc, hs, ht, ws, wt, c, wb, out_0, out
             tr_e(3, j, 1, "s")
             if j > 0:
                 q_e(3, j - 1, 1)
-        pre(0, 0, 256, "v")
+            if j > 1:
+                for h in range(HALVES):
+                    mm_o(3, h, j - 2)
         q_e(3, CHUNKS - 1, 1)
-        pre(0, 256, 512, "v")
-        pre(1, 0, 256, "s")
-        pre(1, 256, 512, "s")
-        for g in range(VG):
+        for g in range(2, VG):
             for h in range(HALVES):
                 mm_o(3, h, g)
-        last(0, "v")
-        last(1, "s")
-        q_f(0, 0, 512)
-        nc.sync.dma_start(out=codes_view[:, 0:CH], in_=fcode[:, 0:CH].bitcast(I32))
-        q_f(1, 0, 512)
-        nc.sync.dma_start(out=codes_view[:, CH:O], in_=fcode[:, CH:O].bitcast(I32))
-        put_o(3, 0, "s")
+        put_o(3, 0, "v")
+        store_o(3, 0)
         put_o(3, 1, "s")
+        store_o(3, 1)
+        il_f(0, 0, 256, "v")
+        il_f(0, 256, 512, "v")
+        il_f(1, 192, 512, "s")
+        q_f(0, 0, 256)
+        put_codes(0, 256)
+        il_f(1, 0, 192, "v")
+        q_f(0, 256, 512)
+        put_codes(256, 512)
+        q_f(1, 0, 256)
+        put_codes(512, 768)
+        q_f(1, 256, 512)
+        put_codes(768, 1024)
         for q in range(4):
             nc.sync.dma_start(
                 out=out_2[0, 4 * q : 4 * q + 4, :].bitcast(I32), in_=fsc[32 * q : 32 * q + 4, :].bitcast(I32)

from contextlib import ExitStack

import concourse.mybir as mybir
from concourse.masks import make_identity

F32 = mybir.dt.float32
BF16 = mybir.dt.bfloat16
U32 = mybir.dt.uint32
I32 = mybir.dt.int32
U8 = mybir.dt.uint8
FP8X4 = mybir.dt.float8_e4m3fn_x4
ACT = mybir.ActivationFunctionType
ALU = mybir.AluOpType
AX = mybir.AxisListType

P = 128
PACK = 4
KP = 512
N, D, V, O = 512, 1024, 2048, 1024
TILES = N // P
CH = 512
CHUNKS = V // CH
DG = D // KP
VG = V // KP
HALVES = O // CH
FLOPS = 2 * N * V * (D + D) + 2 * N * V * O


def tile_jsdlogitgradgainprojection_kernel(tc, hs, ht, ws, wt, c, wb, out_0, out_1, out_2):
    nc = tc.nc
    with ExitStack() as ctx:
        keep = ctx.enter_context(tc.tile_pool(name="keep", bufs=1))
        pool = ctx.enter_context(tc.tile_pool(name="work", bufs=2))
        psum = ctx.enter_context(tc.psum_pool(name="psum", bufs=8))

        ident = keep.tile([P, P], F32, name="ident")
        make_identity(nc, ident[:])

        ctx.enter_context(tc.manual_schedule())

        def bank():
            b = psum.tile([P, KP], F32, name="bank", tag="bank")
            return b

        nmx = keep.tile([P, 32], F32, name="nmx")
        zacc = keep.tile([P, 32], F32, name="zacc")
        ebias = keep.tile([P, 16], F32, name="ebias")

        es = [keep.tile([P, V], F32, name="es%d" % t) for t in range(TILES)]
        ee = [keep.tile([P, V], F32, name="ee%d" % t) for t in range(TILES)]

        raws = {}

        def load_w(x, c_, g, cuts=(0, CH)):
            src = ws if x == 0 else wt
            r = pool.tile([P, PACK, CH], BF16, name="raw", tag="raw", bufs=8, align_bytes=64)
            rows = src[KP * g : KP * (g + 1), CH * c_ : CH * (c_ + 1)].rearrange("(p j) w -> p j w", j=PACK)
            for lo, hi in zip(cuts[:-1], cuts[1:]):
                nc.sync.dma_start(out=r[:, :, lo:hi], in_=rows[:, :, lo:hi])
            raws[x, c_, g] = r

        hraw = [pool.tile([P, TILES, D], BF16, name="hraw%d" % x, tag="big", bufs=2, align_bytes=64) for x in (0, 1)]

        def load_h(x, lo, hi):
            src = (hs if x == 0 else ht).rearrange("(p t) k -> p t k", t=TILES)
            nc.sync.dma_start(out=hraw[x][:, lo:hi, :], in_=src[:, lo:hi, :])

        wbraw = {}

        def load_wb(g):
            r = pool.tile([P, PACK, O], BF16, name="wbraw", tag="wbraw", bufs=2, align_bytes=64)
            nc.sync.dma_start(out=r[:], in_=wb[KP * g : KP * (g + 1), :].rearrange("(p j) w -> p j w", j=PACK))
            wbraw[g] = r

        cb = keep.tile([P, V], BF16, name="cb")

        grps = {}

        def new_grp(key):
            q = pool.tile([P, CH * PACK], BF16, name="grp", tag="grp", bufs=6, align_bytes=64)
            grps[key] = q

        def views(dst, src, lo, hi):
            d = dst[:, PACK * lo : PACK * hi].rearrange("p (c i t) -> p c t i", i=4, t=PACK)
            s = src[:, :, lo:hi].rearrange("p t (c i) -> p c t i", i=4)
            return d, s

        def il_w(x, c_, g, eng, lo=0, hi=CH):
            if (x, c_, g) not in grps:
                new_grp((x, c_, g))
            d, s = views(grps[x, c_, g], raws[x, c_, g], lo, hi)
            if x == 0:
                if eng == "v":
                    nc.vector.tensor_scalar(out=d, in0=s, scalar1=-1.0, scalar2=None, op0=ALU.mult)
                else:
                    nc.scalar.activation(out=d, in_=s, func=ACT.Copy, scale=-1.0)
            elif eng == "v":
                nc.vector.tensor_copy(out=d, in_=s)
            else:
                nc.scalar.copy(out=d, in_=s)

        wcode, wscale = {}, {}

        def alloc_w(x, c_):
            a = pool.tile([P, DG * CH], U32, name="wcode%d" % x, tag="wcode%d" % x, bufs=2, align_bytes=64)
            b = pool.tile([P, DG * CH], U8, name="wscale%d" % x, tag="wscale%d" % x, bufs=2, align_bytes=64)
            wcode[x, c_], wscale[x, c_] = a, b

        def q_w(x, c_, g):
            if (x, c_) not in wcode:
                alloc_w(x, c_)
            cols = slice(CH * g, CH * (g + 1))
            nc.vector.quantize_mx(
                out=wcode[x, c_][:, cols].bitcast(FP8X4), scales=wscale[x, c_][:, cols], in_=grps[x, c_, g][:]
            )

        GP = 128
        gtile = {}

        def g_piece(key, src, i):
            q = pool.tile([P, GP * PACK], BF16, name="gpiece", tag="gpiece", bufs=1, align_bytes=64)
            gtile[key] = q
            d = q[:].rearrange("p (c t) -> p c t", t=PACK)
            s = src[:, :, GP * i : GP * (i + 1)].rearrange("p t c -> p c t")
            nc.gpsimd.tensor_scalar(out=d, in0=s, scalar1=1.0, scalar2=0.0, op0=ALU.mult, op1=ALU.add)

        def g_w(c_, i):
            g_piece((c_, i), raws[1, c_, 1], i)

        def gq_w(c_, i):
            if (1, c_) not in wcode:
                alloc_w(1, c_)
            cols = slice(CH + GP * i, CH + GP * (i + 1))
            nc.vector.quantize_mx(
                out=wcode[1, c_][:, cols].bitcast(FP8X4), scales=wscale[1, c_][:, cols], in_=gtile[c_, i][:]
            )

        def g_b(b_, i):
            g, h = b_ // 2, b_ % 2
            g_piece(("b", b_, i), wbraw[g][:, :, CH * h : CH * (h + 1)], i)

        def gq_b(b_, i):
            g, h = b_ // 2, b_ % 2
            cols = slice(CH * h + GP * i, CH * h + GP * (i + 1))
            nc.vector.quantize_mx(
                out=bcode[g][:, cols].bitcast(FP8X4), scales=bscale[g][:, cols], in_=gtile["b", b_, i][:]
            )

        bcode = [keep.tile([P, O], U32, name="bcode%d" % g, align_bytes=64) for g in range(VG)]
        bscale = [keep.tile([P, O], U8, name="bscale%d" % g, align_bytes=64) for g in range(VG)]

        def il_b(i, eng, lo=0, hi=CH):
            g, h = i // 2, i % 2
            if ("b", i) not in grps:
                new_grp(("b", i))
            d, s = views(grps["b", i], wbraw[g][:, :, CH * h : CH * (h + 1)], lo, hi)
            if eng == "v":
                nc.vector.tensor_copy(out=d, in_=s)
            else:
                nc.scalar.copy(out=d, in_=s)

        def q_b(i):
            g, h = i // 2, i % 2
            cols = slice(CH * h, CH * (h + 1))
            nc.vector.quantize_mx(out=bcode[g][:, cols].bitcast(FP8X4), scales=bscale[g][:, cols], in_=grps["b", i][:])

        hcode, hscale, hgrp = {}, {}, {}

        def tr_h(x, t):
            words = hraw[x][:].bitcast(F32)
            b = bank()
            v = b[:].rearrange("p (g u r) -> p g u r", g=DG, u=2)
            for g in range(DG):
                for u in range(2):
                    nc.tensor.transpose(v[:, g, u, :], words[:, t, 256 * g + u : 256 * (g + 1) : 2], ident[:])
            q = pool.tile([P, DG * P * PACK], BF16, name="hgrp", tag="hgrp", bufs=3, align_bytes=64)
            nc.scalar.copy(
                out=q[:].bitcast(F32).rearrange("p (g r u) -> p g r u", g=DG, u=2),
                in_=b[:].rearrange("p (g u r) -> p g r u", g=DG, u=2),
            )
            hgrp[x, t] = q

        def q_h(x, t):
            a = keep.tile([P, DG * P], U32, name="hcode%d%d" % (x, t), align_bytes=64)
            b = keep.tile([P, DG * P], U8, name="hscale%d%d" % (x, t), align_bytes=64)
            hcode[x, t], hscale[x, t] = a, b
            nc.vector.quantize_mx(out=a[:].bitcast(FP8X4), scales=b[:], in_=hgrp[x, t][:])

        def mm_h(b, x, t, c_, g, start, stop):
            rows = slice(P * g, P * (g + 1))
            cols = slice(CH * g, CH * (g + 1))
            nc.tensor.matmul_mx(
                out=b[:],
                lhsT=hcode[x, t][:, rows].bitcast(FP8X4),
                lhsT_scale=hscale[x, t][:, rows],
                rhs=wcode[x, c_][:, cols].bitcast(FP8X4),
                rhs_scale=wscale[x, c_][:, cols],
                start=start,
                stop=stop,
            )

        units = {}

        def pe_n(t, j):
            b = bank()
            for g in range(DG):
                mm_h(b, 0, t, j, g, g == 0, g == DG - 1)
            units["n", t, j] = b

        def pe_t(t, j):
            b = bank()
            for g in range(DG):
                mm_h(b, 1, t, j, g, g == 0, g == DG - 1)
            units["t", t, j] = b
            b = bank()
            for i, (x, g) in enumerate([(0, 0), (0, 1), (1, 0), (1, 1)]):
                mm_h(b, x, t, j, g, i == 0, i == 3)
            units["d", t, j] = b

        def min_n(t, j):
            k = CHUNKS * t + j
            nc.vector.tensor_reduce(out=nmx[:, k : k + 1], in_=units["n", t, j][:], axis=AX.X, op=ALU.min)

        def max_t(t, j):
            k = CHUNKS * t + j
            nc.vector.tensor_reduce(
                out=nmx[:, 16 + k : 17 + k], in_=units["t", t, j][:], axis=AX.X, op=ALU.max, negate=True
            )

        def ebias_td(t, j):
            k = CHUNKS * t + j
            nc.scalar.activation(
                out=ebias[:, k : k + 1], in_=nmx[:, k : k + 1], func=ACT.Identity, scale=-1.0,
                bias=nmx[:, 16 + k : 17 + k],
            )

        def exp_n(t, j):
            k = CHUNKS * t + j
            cols = slice(CH * j, CH * (j + 1))
            nc.scalar.activation(
                out=es[t][:, cols], in_=units["n", t, j][:], func=ACT.Exp, bias=nmx[:, k : k + 1], scale=-1.0,
                accum_out=zacc[:, k : k + 1],
            )

        def exp_t(t, j):
            k = CHUNKS * t + j
            junk = pool.tile([P, CH], F32, name="junk", tag="junk", bufs=2)
            nc.scalar.activation(
                out=junk[:], in_=units["t", t, j][:], func=ACT.Exp, bias=nmx[:, 16 + k : 17 + k], scale=1.0,
                accum_out=zacc[:, 16 + k : 17 + k],
            )

        def exp_d(t, j):
            k = CHUNKS * t + j
            cols = slice(CH * j, CH * (j + 1))
            nc.scalar.activation(
                out=ee[t][:, cols], in_=units["d", t, j][:], func=ACT.Exp, bias=ebias[:, k : k + 1], scale=1.0
            )

        load_w(0, 0, 0, (0, 256, 512))
        load_w(0, 0, 1)
        load_h(0, 0, 1)
        load_w(1, 0, 0)
        load_h(1, 0, 1)
        load_w(1, 0, 1)
        load_h(0, 1, 2)
        load_h(1, 1, 2)
        load_w(0, 1, 0)
        load_h(0, 2, 3)
        load_h(1, 2, 3)
        load_w(0, 1, 1)
        load_h(0, 3, 4)
        load_h(1, 3, 4)
        load_w(1, 1, 0)
        load_w(1, 1, 1)

        il_w(0, 0, 0, "v", 0, 256)
        il_w(0, 0, 0, "v", 256, 416)
        il_w(0, 0, 0, "s", 416, 512)
        il_w(0, 0, 1, "s", 320, 512)
        q_w(0, 0, 0)
        il_w(0, 0, 1, "v", 0, 320)
        tr_h(0, 0)
        il_w(1, 0, 0, "s", 320, 512)
        il_w(1, 0, 0, "v", 0, 320)
        q_w(0, 0, 1)
        q_h(0, 0)
        tr_h(1, 0)
        pe_n(0, 0)
        q_w(1, 0, 0)
        il_w(1, 0, 1, "v", 0, 320)
        min_n(0, 0)
        il_w(1, 0, 1, "s", 320, 512)
        exp_n(0, 0)
        q_h(1, 0)
        q_w(1, 0, 1)
        tr_h(0, 1)
        tr_h(1, 1)
        q_h(0, 1)

        vfill, sfill, gfill = {}, {}, {}
        for j in range(CHUNKS):
            for t in range(TILES):
                vfill[j, t] = []
                sfill[j, t] = []
                gfill[j, t] = []
        vfill[0, 0] += [lambda: q_h(1, 1), lambda: il_w(0, 1, 0, "v")]
        vfill[0, 1] += [lambda: q_w(0, 1, 0), lambda: q_h(0, 2), lambda: q_h(1, 2), lambda: il_w(0, 1, 1, "v"),
                        lambda: il_w(1, 1, 0, "v", 0, 128)]
        sfill[0, 1] += [lambda: tr_h(0, 3), lambda: tr_h(1, 3)]
        vfill[0, 2] += [lambda: q_h(0, 3), lambda: q_h(1, 3)]
        sfill[0, 1] += [lambda: il_w(1, 1, 0, "s", 128, 512)]
        vfill[0, 2] += [lambda: il_w(1, 1, 1, "v", 0, 384), lambda: q_w(1, 1, 0)]
        sfill[0, 2] += [lambda: il_w(1, 1, 1, "s", 384, 512)]
        vfill[0, 3] += [lambda: q_w(0, 1, 1), lambda: q_w(1, 1, 1)]
        for n in (2, 3):
            slots = [(n - 2, 3), (n - 1, 0), (n - 1, 1), (n - 1, 2)]
            for i, sl in enumerate(slots):
                gfill[sl].append(lambda n=n, i=i: g_w(n, i))
            vfill[slots[0]].append(lambda n=n: il_w(0, n, 0, "v"))
            vfill[slots[1]].append(lambda n=n: il_w(0, n, 1, "v"))
            vfill[slots[2]] += [lambda n=n: q_w(0, n, 0), lambda n=n: q_w(1, n, 0)]
            vfill[slots[3]] += [lambda n=n: q_w(0, n, 1)]
            sfill[slots[0]].append(lambda n=n: il_w(1, n, 0, "s", 0, 224))
            sfill[slots[1]].append(lambda n=n: il_w(1, n, 0, "s", 224, 448))
            vfill[slots[2]].insert(0, lambda n=n: il_w(1, n, 0, "v", 448, 512))
            for i, sl in enumerate(slots):
                vfill[sl].append(lambda n=n, i=i: gq_w(n, i))
        vfill[2, 3] += [lambda: il_b(0, "v")]
        vfill[3, 0] += [lambda: q_b(0)]
        for i in range(4):
            gfill[3, i].append(lambda i=i: g_b(3, i))
            vfill[3, i].append(lambda i=i: gq_b(3, i))

        for j in range(CHUNKS):
            for t in range(TILES):
                if (t, j) != (0, 0):
                    pe_n(t, j)
                    pe_t(t, j)
                    for f in gfill[j, t]:
                        f()
                    min_n(t, j)
                else:
                    pe_t(t, j)
                max_t(t, j)
                if (t, j) != (0, 0):
                    exp_n(t, j)
                ebias_td(t, j)
                if (j, t) == (0, 1):
                    tr_h(0, 2)
                    tr_h(1, 2)
                exp_t(t, j)
                if (j, t) == (CHUNKS - 1, TILES - 1):
                    break
                exp_d(t, j)
                for f in sfill[j, t]:
                    f()
                for f in vfill[j, t]:
                    f()
                if t == 1 and j < 2:
                    for x, g in ((1, 1), (0, 0), (1, 0), (0, 1)):
                        load_w(x, j + 2, g)
                if (j, t) == (1, 2):
                    load_wb(0)
                if (j, t) == (2, 1):
                    load_wb(1)
                if (j, t) == (2, 0):
                    nc.sync.dma_start(out=cb[:], in_=c.partition_broadcast(P))
                if t == 2 and j == 3:
                    load_wb(2)
                    load_wb(3)

        escs = {}

        def es_gain(i):
            e = pool.tile([P, V // 2], F32, name="esc%d" % i, tag="raw", bufs=8, align_bytes=64)
            escs[i] = e
            for h in range(2):
                cols = slice(CH * (2 * i + h), CH * (2 * i + h + 1))
                nc.vector.tensor_tensor(
                    out=e[:, CH * h : CH * (h + 1)], in0=es[3][:, cols], in1=cb[:, cols], op=ALU.mult
                )

        stat = keep.tile([P, 8, 4], F32, name="stat")
        nm = keep.tile([P, 8], F32, name="nm")
        wgt = keep.tile([P, 32], F32, name="wgt")
        zz = keep.tile([P, 32], F32, name="zz")
        zr = keep.tile([P, 8], F32, name="zr")
        rr = keep.tile([P, 8], F32, name="rr")
        gg = keep.tile([P, 32], F32, name="gg")
        gs = keep.tile([P, 32], F32, name="gs")
        rec = keep.tile([P, 16], F32, name="rec")
        kap = keep.tile([P, 16], F32, name="kap")
        ff = keep.tile([P, 16], F32, name="ff")
        nmx3 = nmx[:].rearrange("p (a j) -> p a j", j=4)
        nc.vector.tensor_reduce(out=nm[:], in_=nmx3, axis=AX.X, op=ALU.min)
        gq_b(3, 3)
        nc.vector.tensor_tensor(out=stat[:], in0=nm[:].unsqueeze(2).to_broadcast([P, 8, 4]), in1=nmx3, op=ALU.subtract)
        nc.scalar.activation(out=wgt[:], in_=stat[:].rearrange("p a j -> p (a j)"), func=ACT.Exp)
        exp_d(TILES - 1, CHUNKS - 1)
        il_b(1, "v", 0, 128)
        nc.vector.tensor_tensor(out=zz[:], in0=wgt[:], in1=zacc[:], op=ALU.mult)
        il_b(1, "v", 128, 256)
        nc.vector.tensor_reduce(out=zr[:], in_=zz[:].rearrange("p (a j) -> p a j", j=4), axis=AX.X, op=ALU.add)
        il_b(1, "v", 256, 384)
        nc.vector.reciprocal(out=rr[:], in_=zr[:])
        il_b(1, "v", 384, 512)
        nc.vector.tensor_tensor(
            out=gg[:].rearrange("p (a j) -> p a j", j=4),
            in0=wgt[:].rearrange("p (a j) -> p a j", j=4),
            in1=rr[:].unsqueeze(2).to_broadcast([P, 8, 4]),
            op=ALU.mult,
        )
        nc.vector.tensor_scalar(out=gs[:], in0=gg[:], scalar1=1e-30, scalar2=None, op0=ALU.max)
        nc.vector.reciprocal(out=rec[:], in_=gs[:, 0:16])
        nc.vector.scalar_tensor_tensor(
            out=kap[:], in0=gs[:, 16:32], scalar=0.4 / 0.6, in1=rec[:], op0=ALU.mult, op1=ALU.mult
        )
        nc.vector.tensor_scalar(out=ff[:], in0=gg[:, 0:16], scalar1=-0.6 * V, scalar2=None, op0=ALU.mult)
        acc = keep.tile([P, 16], F32, name="acc")
        nmu = keep.tile([P, TILES], F32, name="nmu")
        osb = [pool.tile([P, TILES, CH], F32, name="osb%d" % h, tag="wbraw", bufs=2, align_bytes=64) for h in range(HALVES)]
        pts, xcs, ecode, escale = {}, {}, {}, {}

        def ln(t):
            for j in range(CHUNKS):
                k = CHUNKS * t + j
                cols = slice(CH * j, CH * (j + 1))
                nc.scalar.activation(
                    out=ee[t][:, cols], in_=ee[t][:, cols], func=ACT.Ln, bias=1.0, scale=kap[:, k : k + 1]
                )

        def prod(t):
            p = pool.tile([P, V], F32, name="pt", tag="big", bufs=2, align_bytes=64)
            pts[t] = p
            for j in range(CHUNKS):
                k = CHUNKS * t + j
                cols = slice(CH * j, CH * (j + 1))
                nc.vector.scalar_tensor_tensor(
                    out=p[:, cols], in0=ee[t][:, cols], scalar=80.0, in1=es[t][:, cols], op0=ALU.min, op1=ALU.mult,
                    accum_out=acc[:, k : k + 1],
                )

        def mean(t):
            j4 = pool.tile([P, 4], F32, name="j4", tag="j4", bufs=2)
            nc.vector.scalar_tensor_tensor(
                out=j4[:], in0=acc[:, 4 * t : 4 * t + 4], scalar=-1.0, in1=gg[:, 4 * t : 4 * t + 4],
                op0=ALU.mult, op1=ALU.mult, accum_out=nmu[:, t : t + 1],
            )

        nmf = keep.tile([P, 4], F32, name="nmf")

        def shift3():
            nc.vector.tensor_scalar(
                out=nmf[:], in0=ff[:, 12:16], scalar1=nmu[:, 3:4], scalar2=None, op0=ALU.mult
            )

        def scale3():
            for j in range(CHUNKS):
                cols = slice(CH * j, CH * (j + 1))
                nc.scalar.activation(
                    out=ee[3][:, cols], in_=ee[3][:, cols], func=ACT.Identity, scale=ff[:, 12 + j : 13 + j],
                    bias=nmf[:, j : j + 1],
                )

        def gain3(j):
            if j == 0:
                xc = pool.tile([P, V], BF16, name="xc", tag="raw", bufs=8, align_bytes=64)
                xcs[3] = xc
            cols = slice(CH * j, CH * (j + 1))
            nc.vector.scalar_tensor_tensor(
                out=xcs[3][:, cols], in0=ee[3][:, cols], scalar=-1e30, in1=escs[j // 2][:, CH * (j % 2) : CH * (j % 2 + 1)],
                op0=ALU.max, op1=ALU.mult,
            )

        def centre(t):
            for i in (0, 1):
                cols = slice(1024 * i, 1024 * (i + 1))
                nc.vector.scalar_tensor_tensor(
                    out=pts[t][:, cols], in0=es[t][:, cols], scalar=nmu[:, t : t + 1], in1=pts[t][:, cols],
                    op0=ALU.mult, op1=ALU.add,
                )

        def gain(t, j):
            if j == 0:
                xc = pool.tile([P, V], BF16, name="xc", tag="raw", bufs=8, align_bytes=64)
                xcs[t] = xc
            k = CHUNKS * t + j
            cols = slice(CH * j, CH * (j + 1))
            nc.vector.scalar_tensor_tensor(
                out=xcs[t][:, cols], in0=pts[t][:, cols], scalar=ff[:, k : k + 1], in1=cb[:, cols],
                op0=ALU.mult, op1=ALU.mult,
            )

        egrp = {}

        def tr_e(t, i, n, eng):
            words = xcs[t][:].bitcast(F32)
            b = bank()
            w = n * 2 * P
            v = b[:, :w].rearrange("p (g u r) -> p g u r", g=n, u=2)
            for gi in range(n):
                g = i + gi
                for u in range(2):
                    nc.tensor.transpose(v[:, gi, u, :], words[:, 256 * g + u : 256 * (g + 1) : 2], ident[:])
            q = pool.tile([P, 2 * P * PACK], BF16, name="egrp", tag="hgrp", bufs=3, align_bytes=64)
            o = q[:].bitcast(F32)[:, :w].rearrange("p (g r u) -> p g r u", g=n, u=2)
            s = b[:, :w].rearrange("p (g u r) -> p g r u", g=n, u=2)
            if eng == "s":
                nc.scalar.copy(out=o, in_=s)
            else:
                nc.vector.tensor_copy(out=o, in_=s)
            egrp[t, i] = q

        def q_e(t, i, n):
            if t not in ecode:
                a = pool.tile([P, VG * P], U32, name="ecode", tag="ecode", bufs=3, align_bytes=64)
                b = pool.tile([P, VG * P], U8, name="escale", tag="escale", bufs=3, align_bytes=64)
                ecode[t], escale[t] = a, b
            cols = slice(P * i, P * (i + n))
            nc.vector.quantize_mx(
                out=ecode[t][:, cols].bitcast(FP8X4), scales=escale[t][:, cols], in_=egrp[t, i][:, : n * P * PACK]
            )

        obank = {}

        def mm_o(t, h, g):
            if g == 0:
                obank[t, h] = bank()
            rows = slice(P * g, P * (g + 1))
            cols = slice(CH * h, CH * (h + 1))
            nc.tensor.matmul_mx(
                out=obank[t, h][:],
                lhsT=ecode[t][:, rows].bitcast(FP8X4),
                lhsT_scale=escale[t][:, rows],
                rhs=bcode[g][:, cols].bitcast(FP8X4),
                rhs_scale=bscale[g][:, cols],
                start=(g == 0),
                stop=(g == VG - 1),
            )

        out_view = out_0.rearrange("(p t) m -> p t m", t=TILES)

        def store_o(t, h):
            nc.sync.dma_start(out=out_view[:, t, CH * h : CH * (h + 1)], in_=osb[h][:, t, :])

        def put_o(t, h, eng):
            if eng == "s":
                nc.scalar.copy(out=osb[h][:, t, :], in_=obank[t, h][:])
            else:
                nc.vector.tensor_copy(out=osb[h][:, t, :], in_=obank[t, h][:])
            if t < TILES - 1:
                store_o(t, h)

        def project_h(t, h):
            for g in range(VG):
                mm_o(t, h, g)

        def project(t):
            for h in range(HALVES):
                for g in range(VG):
                    mm_o(t, h, g)

        ln(0)
        il_b(2, "s")
        ln(1)
        il_b(4, "s")
        q_b(1)
        prod(0)
        mean(0)
        centre(0)
        for j in range(CHUNKS):
            gain(0, j)
        tr_e(0, 0, 2, "s")
        tr_e(0, 2, 2, "s")
        il_b(6, "s")
        ln(2)
        il_b(5, "s")
        q_b(2)
        prod(1)
        q_b(4)
        mean(1)
        q_e(0, 0, 2)
        q_e(0, 2, 2)
        centre(1)
        q_b(6)
        project_h(0, 0)
        for j in range(CHUNKS):
            gain(1, j)
        tr_e(1, 0, 2, "s")
        tr_e(1, 2, 2, "s")
        put_o(0, 0, "s")
        il_b(7, "s")
        ln(3)
        prod(2)
        q_b(5)
        mean(2)
        q_e(1, 0, 2)
        q_e(1, 2, 2)
        project_h(1, 0)
        centre(2)
        q_b(7)
        project_h(0, 1)
        put_o(1, 0, "s")
        put_o(0, 1, "s")
        for j in range(CHUNKS):
            gain(2, j)
        tr_e(2, 0, 2, "s")
        tr_e(2, 2, 2, "s")
        project_h(1, 1)
        put_o(1, 1, "s")
        prod(3)
        q_e(2, 0, 2)
        mean(3)
        q_e(2, 2, 2)
        project_h(2, 0)
        centre(3)
        fsc = keep.tile([P, O], U8, name="fsc", align_bytes=64)
        fcode = keep.tile([P, O], U32, name="fcode", align_bytes=64)
        fg = [pool.tile([P, CH * PACK], BF16, name="fg%d" % h, tag="grp", bufs=6, align_bytes=64) for h in range(HALVES)]

        def q_f(h, lo, hi):
            cols = slice(CH * h + lo, CH * h + hi)
            nc.vector.quantize_mx(
                out=fcode[:, cols].bitcast(FP8X4), scales=fsc[:, cols], in_=fg[h][:, PACK * lo : PACK * hi]
            )

        def il_f(h, lo, hi, eng):
            d, s = views(fg[h], osb[h], lo, hi)
            if eng == "v":
                nc.vector.tensor_copy(out=d, in_=s)
            else:
                nc.scalar.copy(out=d, in_=s)

        codes_view = out_1[0].rearrange("p m t -> p (m t)").bitcast(I32)

        def put_codes(lo, hi):
            nc.sync.dma_start(out=codes_view[:, lo:hi], in_=fcode[:, lo:hi].bitcast(I32))

        project_h(2, 1)
        put_o(2, 0, "s")
        put_o(2, 1, "s")
        for j in range(CHUNKS):
            gain(3, j)
            tr_e(3, j, 1, "s")
            if j > 0:
                q_e(3, j - 1, 1)
            if j > 1:
                for h in range(HALVES):
                    mm_o(3, h, j - 2)
        q_e(3, CHUNKS - 1, 1)
        for g in range(2, VG):
            for h in range(HALVES):
                mm_o(3, h, g)
        put_o(3, 0, "v")
        store_o(3, 0)
        put_o(3, 1, "s")
        store_o(3, 1)
        il_f(0, 0, 256, "v")
        il_f(0, 256, 512, "v")
        il_f(1, 192, 512, "s")
        q_f(0, 0, 256)
        put_codes(0, 256)
        il_f(1, 0, 192, "v")
        q_f(0, 256, 512)
        put_codes(256, 512)
        q_f(1, 0, 256)
        put_codes(512, 768)
        q_f(1, 256, 512)
        put_codes(768, 1024)
        for q in range(4):
            nc.sync.dma_start(
                out=out_2[0, 4 * q : 4 * q + 4, :].bitcast(I32), in_=fsc[32 * q : 32 * q + 4, :].bitcast(I32)
            )
